import numpy as np
import ml_dtypes


def mxq(x, axis, fmt="e4m3"):
    dtype, down = {"e4m3": (ml_dtypes.float8_e4m3fn, 7), "e5m2": (ml_dtypes.float8_e5m2, 14)}[fmt]
    v = np.moveaxis(np.asarray(x, np.float32).astype(ml_dtypes.bfloat16).astype(np.float64), axis, -1)
    blocks = v.reshape(v.shape[:-1] + (-1, 32))
    amax = np.abs(blocks).max(-1, keepdims=True)
    byte = np.maximum(np.where(amax > 0, np.frexp(amax)[1] - 1 + 127, 0) - down, 1)
    scale = np.exp2(byte - 127.0)
    codes = (blocks / scale).astype(np.float32).astype(dtype).astype(np.float64)
    return np.moveaxis((codes * scale).reshape(v.shape), -1, axis)


WIDE = False


def mx_kscale(k):
    if not WIDE:
        return np.ones(k)
    levels = np.array([10, -10, 5, -5, 0])
    if k % 512:
        return np.exp2(np.random.permutation(np.resize(levels, k // 32))).repeat(32)
    a = np.empty((k // 512, 16))
    for p in range(k // 512):
        a[p, :8] = np.random.permutation(np.resize(levels, 8))
        for g in range(8):
            far = levels[np.abs(levels - a[p, g]) >= 10]
            a[p, g + 8] = far[np.random.randint(len(far))]
    return np.exp2(a.ravel()).repeat(32)


def f64(x):
    return np.asarray(x).astype(np.float64)


def striped(idx):
    return np.tile(idx.reshape(-1, 16).T, (8, 1)).astype(np.uint16)


def unstriped(offs):
    return offs[:16].T.reshape(-1).astype(np.int64)


def relu(v):
    return np.maximum(v, 0.0)


K, T, D, S, V, N = 512, 4096, 4, 1024, 256, 512


def setup_inputs():
    n = np.random.standard_normal
    s = mx_kscale(K)[:, None]
    return {
        "xT": (n((K, T)) * s).astype(np.float32),
        "w": (n((K, N)) / np.sqrt(K) / s).astype(np.float32),
        "b": (0.3 * n((N, 1))).astype(np.float32),
        "offs": striped(np.random.permutation(T)[:S]),
    }


def reference(xT, w, b, offs):
    idx = unstriped(offs)
    xq = mxq(f64(xT)[:, idx], 0, "e4m3")
    y = mxq(f64(w), 0, "e4m3").T @ xq
    y = relu(y + f64(b))
    return y.reshape(N, V, D).max(axis=2)

@@ -1,0 +1,203 @@
+from contextlib import ExitStack
+
+import concourse.mybir as mybir
+
+K, T, D, S, N = 512, 4096, 4, 1024, 512
+V = S // D
+FLOPS = 2 * K * N * S
+
+F32 = mybir.dt.float32
+BF16 = mybir.dt.bfloat16
+U32 = mybir.dt.uint32
+U16 = mybir.dt.uint16
+U8 = mybir.dt.uint8
+FP8X4 = mybir.dt.float8_e4m3fn_x4
+COPY = mybir.ActivationFunctionType.Copy
+IDENTITY = mybir.ActivationFunctionType.Identity
+ADD = mybir.AluOpType.add
+MAX = mybir.AluOpType.max
+
+P = 128
+HALF = S // 2
+VH = V // 2
+MT = N // P
+
+CHUNKS = (
+    ((0, 2048, 1280), (2048, 2048, 1280)),
+    ((0, 2048, 1280), (2048, 1024, 640), (3072, 768, 480), (3840, 256, 256)),
+)
+
+
+def tile_picked_pool_lin_relu_sub_e_kernel(tc, xT, w, b, offs, out):
+    nc = tc.nc
+    with ExitStack() as ctx:
+        keep = ctx.enter_context(tc.tile_pool(name="keep", bufs=1))
+        psum = ctx.enter_context(tc.psum_pool(name="psum", bufs=1))
+
+        offsets = keep.tile([P, S // 16], U16, name="offsets")
+        nc.sync.dma_start(offsets[:], offs)
+        bias = keep.tile([P, MT], F32, name="bias")
+        nc.scalar.dma_start(out=bias[:], in_=b.rearrange("(t p) o -> p (t o)", p=P))
+
+        x_rows = xT.rearrange("(p j) n -> p j n", j=4)
+        w_rows = w.rearrange("(p j) m -> p j m", j=4)
+        pieces = ((0, 256), (256, 512))
+        w_raws, w_codes, w_scales = [], [], []
+
+        def load_w(i):
+            c0, c1 = pieces[i]
+            r = keep.tile([P, 4, c1 - c0], F32, name=f"w_raw{i}")
+            nc.sync.dma_start(out=r[:], in_=w_rows[:, :, c0:c1])
+            w_raws.append(r)
+
+        def cast_w(i):
+            c0, c1 = pieces[i]
+            g = keep.tile([P, c1 - c0, 4], BF16, name=f"w_groups{i}", align_bytes=64)
+            nc.scalar.activation(out=g[:], in_=w_raws[i][:].rearrange("p j m -> p m j"), func=COPY)
+            return g
+
+        def quantize_w(i, g):
+            c0, c1 = pieces[i]
+            codes = keep.tile([P, c1 - c0], U32, name=f"w_codes{i}", align_bytes=64)
+            scales = keep.tile([P, c1 - c0], U8, name=f"w_scales{i}", align_bytes=64)
+            nc.vector.quantize_mx(
+                out=codes[:].bitcast(FP8X4), scales=scales[:], in_=g[:].rearrange("p m j -> p (m j)")
+            )
+            w_codes.append(codes)
+            w_scales.append(scales)
+
+        raw = []
+        for u in range(2):
+            per_pair = []
+            for c, (n0, width, share) in enumerate(CHUNKS[u]):
+                r = keep.tile([P, 2, width], F32, name=f"raw{u}{c}")
+                nc.sync.dma_start(out=r[:], in_=x_rows[:, 2 * u : 2 * u + 2, n0 : n0 + width])
+                per_pair.append(r)
+                if u == 0 and c == 0:
+                    for i in range(0):
+                        load_w(i)
+            raw.append(per_pair)
+        for i in range(0, len(pieces)):
+            load_w(i)
+
+        pairs = [keep.tile([P, T, 2], BF16, name=f"pairs{u}", align_bytes=64) for u in range(2)]
+        groups = [keep.tile([P, HALF * 4], BF16, name=f"groups{h}", align_bytes=64) for h in range(2)]
+        x_codes = [keep.tile([P, HALF], U32, name=f"x_codes{h}", align_bytes=64) for h in range(2)]
+        x_scales = [keep.tile([P, HALF], U8, name=f"x_scales{h}", align_bytes=64) for h in range(2)]
+
+        def cast_pairs(u, c):
+            n0, width, share = CHUNKS[u][c]
+            r = raw[u][c]
+            if share:
+                nc.vector.tensor_copy(
+                    out=pairs[u][:, n0 : n0 + share, :], in_=r[:, :, 0:share].rearrange("p e n -> p n e")
+                )
+            if share < width:
+                nc.scalar.activation(
+                    out=pairs[u][:, n0 + share : n0 + width, :],
+                    in_=r[:, :, share:width].rearrange("p e n -> p n e"),
+                    func=COPY,
+                )
+
+        def gather(u, h):
+            window = pairs[u][:].rearrange("p n e -> p (n e)").bitcast(U32)
+            picked = groups[h][:].bitcast(U32).rearrange("p (n e) -> p n e", e=2)
+            span = HALF // 16
+            nc.vector.tensor_copy(out=picked[:, :, u], in_=window.indirect(offsets[:, h * span : (h + 1) * span]))
+
+        def quantize(h):
+            nc.vector.quantize_mx(out=x_codes[h][:].bitcast(FP8X4), scales=x_scales[h][:], in_=groups[h][:])
+
+        sums = {}
+
+        def multiply(h, t):
+            acc = psum.tile([P, VH, D], F32, name=f"acc{h}{t}")
+            i = [k for k, (c0, c1) in enumerate(pieces) if c0 <= t * P < c1][0]
+            cols = slice(t * P - pieces[i][0], t * P - pieces[i][0] + P)
+            nc.tensor.matmul_mx(
+                out=acc[:].rearrange("p v d -> p (v d)"),
+                lhsT=w_codes[i][:, cols].bitcast(FP8X4),
+                lhsT_scale=w_scales[i][:, cols],
+                rhs=x_codes[h][:].bitcast(FP8X4),
+                rhs_scale=x_scales[h][:],
+                start=True,
+                stop=True,
+            )
+            sums[h, t] = acc
+
+        out_view = out.rearrange("(t p) v -> p t v", p=P)
+        halves = [keep.tile([P, MT, VH, 2], F32, name=f"halves{h}") for h in range(2)]
+        best = [keep.tile([P, MT, VH], F32, name=f"best{h}") for h in range(2)]
+        first = [keep.tile([P, MT, VH, 2], F32, name=f"first{h}") for h in range(2)]
+
+        def pool_pairs(h, t):
+            acc = sums[h, t]
+            nc.scalar.activation(
+                out=first[h][:, t, :, :], in_=acc[:, :, 0:2], func=IDENTITY, bias=bias[:, t : t + 1], scale=1.0
+            )
+            nc.vector.scalar_tensor_tensor(
+                out=halves[h][:, t, :, :],
+                in0=acc[:, :, 2:4],
+                scalar=bias[:, t : t + 1],
+                in1=first[h][:, t, :, :],
+                op0=ADD,
+                op1=MAX,
+            )
+
+        def pool_all(h, t):
+            most = keep.tile([P, VH], F32, name=f"most{h}{t}")
+            nc.vector.tensor_reduce(out=most[:], in_=sums[h, t][:], axis=mybir.AxisListType.X, op=MAX)
+            nc.vector.tensor_scalar(
+                out=best[h][:, t, :], in0=most[:], scalar1=bias[:, t : t + 1], scalar2=0.0, op0=ADD, op1=MAX
+            )
+
+        def store(h, t0, t1):
+            nc.sync.dma_start(out=out_view[:, t0:t1, h * VH : (h + 1) * VH], in_=best[h][:, t0:t1, :])
+
+        def finish(h, t0, t1):
+            some = slice(t0, t1)
+            nc.vector.scalar_tensor_tensor(
+                out=best[h][:, some, :],
+                in0=halves[h][:, some, :, 0],
+                scalar=0.0,
+                in1=halves[h][:, some, :, 1],
+                op0=MAX,
+                op1=MAX,
+            )
+
+        cast_pairs(0, 0)
+        cast_pairs(0, 1)
+        gather(0, 0)
+        gather(0, 1)
+        for c in range(len(CHUNKS[1])):
+            cast_pairs(1, c)
+        gather(1, 0)
+        gather(1, 1)
+        w_groups = [cast_w(i) for i in range(2)]
+        quantize_w(0, w_groups[0])
+        quantize(0)
+        multiply(0, 0)
+        multiply(0, 1)
+        quantize(1)
+        quantize_w(1, w_groups[1])
+        multiply(0, 2)
+        multiply(0, 3)
+        for t in range(MT):
+            multiply(1, t)
+
+        pool_all(0, 0)
+        pool_pairs(0, 1)
+        pool_pairs(0, 2)
+        finish(0, 1, 3)
+        store(0, 0, 3)
+        pool_pairs(0, 3)
+        pool_pairs(1, 0)
+        finish(0, 3, 4)
+        store(0, 3, 4)
+        pool_pairs(1, 1)
+        finish(1, 0, 2)
+        store(1, 0, 2)
+        pool_pairs(1, 2)
+        finish(1, 2, 3)
+        pool_all(1, 3)
+        store(1, 2, 4)

@@ -24,7 +24,7 @@ MT = N // P
 
 CHUNKS = (
     ((0, 2048, 1280), (2048, 2048, 1280)),
-    ((0, 2048, 1280), (2048, 1024, 640), (3072, 768, 480), (3840, 256, 256)),
+    ((0, 2048, 1280), (2048, 1024, 640), (3072, 768, 480), (3840, 256, 176)),
 )
 
 
@@ -37,7 +37,6 @@ def tile_picked_pool_lin_relu_sub_e_kernel(tc, xT, w, b, offs, out):
         offsets = keep.tile([P, S // 16], U16, name="offsets")
         nc.sync.dma_start(offsets[:], offs)
         bias = keep.tile([P, MT], F32, name="bias")
-        nc.scalar.dma_start(out=bias[:], in_=b.rearrange("(t p) o -> p (t o)", p=P))
 
         x_rows = xT.rearrange("(p j) n -> p j n", j=4)
         w_rows = w.rearrange("(p j) m -> p j m", j=4)
@@ -50,10 +49,9 @@ def tile_picked_pool_lin_relu_sub_e_kernel(tc, xT, w, b, offs, out):
             nc.sync.dma_start(out=r[:], in_=w_rows[:, :, c0:c1])
             w_raws.append(r)
 
-        def cast_w(i):
-            c0, c1 = pieces[i]
-            g = keep.tile([P, c1 - c0, 4], BF16, name=f"w_groups{i}", align_bytes=64)
-            nc.scalar.activation(out=g[:], in_=w_raws[i][:].rearrange("p j m -> p m j"), func=COPY)
+        def cast_w(i, g):
+            view = g.rearrange("p (m j) -> p m j", j=4)
+            nc.scalar.activation(out=view, in_=w_raws[i][:].rearrange("p j m -> p m j"), func=COPY)
             return g
 
         def quantize_w(i, g):
@@ -61,7 +59,7 @@ def tile_picked_pool_lin_relu_sub_e_kernel(tc, xT, w, b, offs, out):
             codes = keep.tile([P, c1 - c0], U32, name=f"w_codes{i}", align_bytes=64)
             scales = keep.tile([P, c1 - c0], U8, name=f"w_scales{i}", align_bytes=64)
             nc.vector.quantize_mx(
-                out=codes[:].bitcast(FP8X4), scales=scales[:], in_=g[:].rearrange("p m j -> p (m j)")
+                out=codes[:].bitcast(FP8X4), scales=scales[:], in_=g
             )
             w_codes.append(codes)
             w_scales.append(scales)
@@ -73,15 +71,18 @@ def tile_picked_pool_lin_relu_sub_e_kernel(tc, xT, w, b, offs, out):
                 r = keep.tile([P, 2, width], F32, name=f"raw{u}{c}")
                 nc.sync.dma_start(out=r[:], in_=x_rows[:, 2 * u : 2 * u + 2, n0 : n0 + width])
                 per_pair.append(r)
-                if u == 0 and c == 0:
-                    for i in range(0):
-                        load_w(i)
             raw.append(per_pair)
         for i in range(0, len(pieces)):
             load_w(i)
+        nc.sync.dma_start(out=bias[:], in_=b.rearrange("(t p) o -> p (t o)", p=P))
 
         pairs = [keep.tile([P, T, 2], BF16, name=f"pairs{u}", align_bytes=64) for u in range(2)]
-        groups = [keep.tile([P, HALF * 4], BF16, name=f"groups{h}", align_bytes=64) for h in range(2)]
+        W_WIDE = 256 * 4
+        X_WIDE = HALF * 4
+        picks0 = keep.tile([P, X_WIDE], BF16, name="picks0", align_bytes=64)
+        shared = keep.tile([P, W_WIDE + X_WIDE], BF16, name="shared", align_bytes=64)
+        w_last = keep.tile([P, W_WIDE], BF16, name="w_last", align_bytes=64)
+        picks = [picks0[:], shared[:, W_WIDE:]]
         x_codes = [keep.tile([P, HALF], U32, name=f"x_codes{h}", align_bytes=64) for h in range(2)]
         x_scales = [keep.tile([P, HALF], U8, name=f"x_scales{h}", align_bytes=64) for h in range(2)]
 
@@ -99,19 +100,18 @@ def tile_picked_pool_lin_relu_sub_e_kernel(tc, xT, w, b, offs, out):
                     func=COPY,
                 )
 
-        def gather(u, h):
+        def gather(u, j0, j1, where):
             window = pairs[u][:].rearrange("p n e -> p (n e)").bitcast(U32)
-            picked = groups[h][:].bitcast(U32).rearrange("p (n e) -> p n e", e=2)
-            span = HALF // 16
-            nc.vector.tensor_copy(out=picked[:, :, u], in_=window.indirect(offsets[:, h * span : (h + 1) * span]))
+            picked = where.bitcast(U32).rearrange("p (n e) -> p n e", e=2)
+            nc.vector.tensor_copy(out=picked[:, :, u], in_=window.indirect(offsets[:, j0 // 16 : j1 // 16]))
 
         def quantize(h):
-            nc.vector.quantize_mx(out=x_codes[h][:].bitcast(FP8X4), scales=x_scales[h][:], in_=groups[h][:])
+            nc.vector.quantize_mx(out=x_codes[h][:].bitcast(FP8X4), scales=x_scales[h][:], in_=picks[h])
 
         sums = {}
 
-        def multiply(h, t):
-            acc = psum.tile([P, VH, D], F32, name=f"acc{h}{t}")
+        def multiply(h, t, into=None):
+            acc = into or psum.tile([P, VH, D], F32, name=f"acc{h}{t}")
             i = [k for k, (c0, c1) in enumerate(pieces) if c0 <= t * P < c1][0]
             cols = slice(t * P - pieces[i][0], t * P - pieces[i][0] + P)
             nc.tensor.matmul_mx(
@@ -123,7 +123,8 @@ def tile_picked_pool_lin_relu_sub_e_kernel(tc, xT, w, b, offs, out):
                 start=True,
                 stop=True,
             )
-            sums[h, t] = acc
+            if not into:
+                sums[h, t] = acc
 
         out_view = out.rearrange("(t p) v -> p t v", p=P)
         halves = [keep.tile([P, MT, VH, 2], F32, name=f"halves{h}") for h in range(2)]
@@ -144,13 +145,6 @@ def tile_picked_pool_lin_relu_sub_e_kernel(tc, xT, w, b, offs, out):
                 op1=MAX,
             )
 
-        def pool_all(h, t):
-            most = keep.tile([P, VH], F32, name=f"most{h}{t}")
-            nc.vector.tensor_reduce(out=most[:], in_=sums[h, t][:], axis=mybir.AxisListType.X, op=MAX)
-            nc.vector.tensor_scalar(
-                out=best[h][:, t, :], in0=most[:], scalar1=bias[:, t : t + 1], scalar2=0.0, op0=ADD, op1=MAX
-            )
-
         def store(h, t0, t1):
             nc.sync.dma_start(out=out_view[:, t0:t1, h * VH : (h + 1) * VH], in_=best[h][:, t0:t1, :])
 
@@ -167,37 +161,37 @@ def tile_picked_pool_lin_relu_sub_e_kernel(tc, xT, w, b, offs, out):
 
         cast_pairs(0, 0)
         cast_pairs(0, 1)
-        gather(0, 0)
-        gather(0, 1)
+        gather(0, 0, HALF, picks[0])
+        gather(0, HALF, S, picks[1])
         for c in range(len(CHUNKS[1])):
             cast_pairs(1, c)
-        gather(1, 0)
-        gather(1, 1)
-        w_groups = [cast_w(i) for i in range(2)]
-        quantize_w(0, w_groups[0])
+        gather(1, 0, HALF, picks[0])
+        w_groups = [cast_w(0, shared[:, 0:W_WIDE]), cast_w(1, w_last[:])]
         quantize(0)
+        quantize_w(0, w_groups[0])
         multiply(0, 0)
         multiply(0, 1)
-        quantize(1)
+        for t in range(2):
+            sums[1, 2 + t] = psum.tile([P, VH, D], F32, name=f"acc1{2 + t}")
+            multiply(0, t, sums[1, 2 + t])
+        gather(1, HALF - 32, S, shared[:, W_WIDE - 32 * 4 :])
         quantize_w(1, w_groups[1])
         multiply(0, 2)
         multiply(0, 3)
+        quantize(1)
+        multiply(1, 0)
+        multiply(1, 1)
+        multiply(1, 2, sums[1, 2])
+        multiply(1, 3, sums[1, 3])
         for t in range(MT):
-            multiply(1, t)
-
-        pool_all(0, 0)
-        pool_pairs(0, 1)
-        pool_pairs(0, 2)
-        finish(0, 1, 3)
-        store(0, 0, 3)
-        pool_pairs(0, 3)
+            pool_pairs(0, t)
         pool_pairs(1, 0)
-        finish(0, 3, 4)
-        store(0, 3, 4)
+        finish(0, 0, 4)
+        store(0, 0, 4)
         pool_pairs(1, 1)
+        pool_pairs(1, 2)
         finish(1, 0, 2)
         store(1, 0, 2)
-        pool_pairs(1, 2)
-        finish(1, 2, 3)
-        pool_all(1, 3)
+        pool_pairs(1, 3)
+        finish(1, 2, 4)
         store(1, 2, 4)

@@ -22,10 +22,7 @@ HALF = S // 2
 VH = V // 2
 MT = N // P
 
-CHUNKS = (
-    ((0, 2048, 1280), (2048, 2048, 1280)),
-    ((0, 2048, 1280), (2048, 1024, 640), (3072, 768, 480), (3840, 256, 176)),
-)
+CHUNKS = ((0, 2048, 1280), (2048, 2048, 1280))
 
 
 def tile_picked_pool_lin_relu_sub_e_kernel(tc, xT, w, b, offs, out):
@@ -65,18 +62,20 @@ def tile_picked_pool_lin_relu_sub_e_kernel(tc, xT, w, b, offs, out):
             w_scales.append(scales)
 
         raw = []
-        for u in range(2):
-            per_pair = []
-            for c, (n0, width, share) in enumerate(CHUNKS[u]):
-                r = keep.tile([P, 2, width], F32, name=f"raw{u}{c}")
-                nc.sync.dma_start(out=r[:], in_=x_rows[:, 2 * u : 2 * u + 2, n0 : n0 + width])
-                per_pair.append(r)
-            raw.append(per_pair)
+        for c, (n0, width, share) in enumerate(CHUNKS):
+            r = keep.tile([P, 2, width], F32, name=f"raw{c}")
+            nc.sync.dma_start(out=r[:], in_=x_rows[:, 0:2, n0 : n0 + width])
+            raw.append(r)
+        planes = []
+        for j in range(2, 4):
+            r = keep.tile([P, T], F32, name=f"plane{j}")
+            nc.sync.dma_start(out=r[:], in_=x_rows[:, j, :])
+            planes.append(r)
         for i in range(0, len(pieces)):
             load_w(i)
         nc.sync.dma_start(out=bias[:], in_=b.rearrange("(t p) o -> p (t o)", p=P))
 
-        pairs = [keep.tile([P, T, 2], BF16, name=f"pairs{u}", align_bytes=64) for u in range(2)]
+        pairs = keep.tile([P, T, 2], BF16, name="pairs", align_bytes=64)
         W_WIDE = 256 * 4
         X_WIDE = HALF * 4
         picks0 = keep.tile([P, X_WIDE], BF16, name="picks0", align_bytes=64)
@@ -86,24 +85,25 @@ def tile_picked_pool_lin_relu_sub_e_kernel(tc, xT, w, b, offs, out):
         x_codes = [keep.tile([P, HALF], U32, name=f"x_codes{h}", align_bytes=64) for h in range(2)]
         x_scales = [keep.tile([P, HALF], U8, name=f"x_scales{h}", align_bytes=64) for h in range(2)]
 
-        def cast_pairs(u, c):
-            n0, width, share = CHUNKS[u][c]
-            r = raw[u][c]
-            if share:
-                nc.vector.tensor_copy(
-                    out=pairs[u][:, n0 : n0 + share, :], in_=r[:, :, 0:share].rearrange("p e n -> p n e")
-                )
-            if share < width:
-                nc.scalar.activation(
-                    out=pairs[u][:, n0 + share : n0 + width, :],
-                    in_=r[:, :, share:width].rearrange("p e n -> p n e"),
-                    func=COPY,
-                )
+        def cast_pairs(c):
+            n0, width, share = CHUNKS[c]
+            nc.vector.tensor_copy(
+                out=pairs[:, n0 : n0 + share, :], in_=raw[c][:, :, 0:share].rearrange("p e n -> p n e")
+            )
+            nc.scalar.activation(
+                out=pairs[:, n0 + share : n0 + width, :],
+                in_=raw[c][:, :, share:width].rearrange("p e n -> p n e"),
+                func=COPY,
+            )
 
-        def gather(u, j0, j1, where):
-            window = pairs[u][:].rearrange("p n e -> p (n e)").bitcast(U32)
+        def gather_pairs(j0, j1, where):
+            window = pairs[:].rearrange("p n e -> p (n e)").bitcast(U32)
             picked = where.bitcast(U32).rearrange("p (n e) -> p n e", e=2)
-            nc.vector.tensor_copy(out=picked[:, :, u], in_=window.indirect(offsets[:, j0 // 16 : j1 // 16]))
+            nc.vector.tensor_copy(out=picked[:, :, 0], in_=window.indirect(offsets[:, j0 // 16 : j1 // 16]))
+
+        def gather_plane(j, j0, j1, where):
+            picked = where.rearrange("p (n t) -> p n t", t=4)
+            nc.vector.tensor_copy(out=picked[:, :, j], in_=planes[j - 2][:].indirect(offsets[:, j0 // 16 : j1 // 16]))
 
         def quantize(h):
             nc.vector.quantize_mx(out=x_codes[h][:].bitcast(FP8X4), scales=x_scales[h][:], in_=picks[h])
@@ -159,13 +159,13 @@ def tile_picked_pool_lin_relu_sub_e_kernel(tc, xT, w, b, offs, out):
                 op1=MAX,
             )
 
-        cast_pairs(0, 0)
-        cast_pairs(0, 1)
-        gather(0, 0, HALF, picks[0])
-        gather(0, HALF, S, picks[1])
-        for c in range(len(CHUNKS[1])):
-            cast_pairs(1, c)
-        gather(1, 0, HALF, picks[0])
+        cast_pairs(0)
+        cast_pairs(1)
+        gather_pairs(0, HALF, picks[0])
+        gather_pairs(HALF, S, picks[1])
+        gather_plane(2, 0, HALF, picks[0])
+        gather_plane(2, HALF, S, picks[1])
+        gather_plane(3, 0, HALF, picks[0])
         w_groups = [cast_w(0, shared[:, 0:W_WIDE]), cast_w(1, w_last[:])]
         quantize(0)
         quantize_w(0, w_groups[0])
@@ -174,7 +174,7 @@ def tile_picked_pool_lin_relu_sub_e_kernel(tc, xT, w, b, offs, out):
         for t in range(2):
             sums[1, 2 + t] = psum.tile([P, VH, D], F32, name=f"acc1{2 + t}")
             multiply(0, t, sums[1, 2 + t])
-        gather(1, HALF - 32, S, shared[:, W_WIDE - 32 * 4 :])
+        gather_plane(3, HALF - 32, S, shared[:, W_WIDE - 32 * 4 :])
         quantize_w(1, w_groups[1])
         multiply(0, 2)
         multiply(0, 3)

@@ -22,8 +22,6 @@ HALF = S // 2
 VH = V // 2
 MT = N // P
 
-CHUNKS = ((0, 2048, 1280), (2048, 2048, 1280))
-
 
 def tile_picked_pool_lin_relu_sub_e_kernel(tc, xT, w, b, offs, out):
     nc = tc.nc
@@ -37,18 +35,17 @@ def tile_picked_pool_lin_relu_sub_e_kernel(tc, xT, w, b, offs, out):
 
         x_rows = xT.rearrange("(p j) n -> p j n", j=4)
         w_rows = w.rearrange("(p j) m -> p j m", j=4)
-        pieces = ((0, 256), (256, 512))
-        w_raws, w_codes, w_scales = [], [], []
+        pieces = ((0, 128), (128, 256), (256, 512))
+        w_codes, w_scales = [], []
 
-        def load_w(i):
-            c0, c1 = pieces[i]
-            r = keep.tile([P, 4, c1 - c0], F32, name=f"w_raw{i}")
+        def load_w(c0, c1, name):
+            r = keep.tile([P, 4, c1 - c0], F32, name=name)
             nc.sync.dma_start(out=r[:], in_=w_rows[:, :, c0:c1])
-            w_raws.append(r)
+            return r
 
         def cast_w(i, g):
             view = g.rearrange("p (m j) -> p m j", j=4)
-            nc.scalar.activation(out=view, in_=w_raws[i][:].rearrange("p j m -> p m j"), func=COPY)
+            nc.scalar.activation(out=view, in_=w_raws[i].rearrange("p j m -> p m j"), func=COPY)
             return g
 
         def quantize_w(i, g):
@@ -61,49 +58,28 @@ def tile_picked_pool_lin_relu_sub_e_kernel(tc, xT, w, b, offs, out):
             w_codes.append(codes)
             w_scales.append(scales)
 
-        raw = []
-        for c, (n0, width, share) in enumerate(CHUNKS):
-            r = keep.tile([P, 2, width], F32, name=f"raw{c}")
-            nc.sync.dma_start(out=r[:], in_=x_rows[:, 0:2, n0 : n0 + width])
-            raw.append(r)
         planes = []
-        for j in range(2, 4):
+        for j in range(4):
             r = keep.tile([P, T], F32, name=f"plane{j}")
             nc.sync.dma_start(out=r[:], in_=x_rows[:, j, :])
             planes.append(r)
-        for i in range(0, len(pieces)):
-            load_w(i)
+        w_front = load_w(0, 256, "w_front")
+        w_back = load_w(256, 512, "w_back")
+        w_raws = [w_front[:, :, 0:128], w_front[:, :, 128:256], w_back[:]]
         nc.sync.dma_start(out=bias[:], in_=b.rearrange("(t p) o -> p (t o)", p=P))
 
-        pairs = keep.tile([P, T, 2], BF16, name="pairs", align_bytes=64)
-        W_WIDE = 256 * 4
+        W_WIDE = 128 * 4
         X_WIDE = HALF * 4
         picks0 = keep.tile([P, X_WIDE], BF16, name="picks0", align_bytes=64)
         shared = keep.tile([P, W_WIDE + X_WIDE], BF16, name="shared", align_bytes=64)
-        w_last = keep.tile([P, W_WIDE], BF16, name="w_last", align_bytes=64)
+        w_rest = [keep.tile([P, n * 4], BF16, name=f"w_rest{n}", align_bytes=64) for n in (128, 256)]
         picks = [picks0[:], shared[:, W_WIDE:]]
         x_codes = [keep.tile([P, HALF], U32, name=f"x_codes{h}", align_bytes=64) for h in range(2)]
         x_scales = [keep.tile([P, HALF], U8, name=f"x_scales{h}", align_bytes=64) for h in range(2)]
 
-        def cast_pairs(c):
-            n0, width, share = CHUNKS[c]
-            nc.vector.tensor_copy(
-                out=pairs[:, n0 : n0 + share, :], in_=raw[c][:, :, 0:share].rearrange("p e n -> p n e")
-            )
-            nc.scalar.activation(
-                out=pairs[:, n0 + share : n0 + width, :],
-                in_=raw[c][:, :, share:width].rearrange("p e n -> p n e"),
-                func=COPY,
-            )
-
-        def gather_pairs(j0, j1, where):
-            window = pairs[:].rearrange("p n e -> p (n e)").bitcast(U32)
-            picked = where.bitcast(U32).rearrange("p (n e) -> p n e", e=2)
-            nc.vector.tensor_copy(out=picked[:, :, 0], in_=window.indirect(offsets[:, j0 // 16 : j1 // 16]))
-
         def gather_plane(j, j0, j1, where):
             picked = where.rearrange("p (n t) -> p n t", t=4)
-            nc.vector.tensor_copy(out=picked[:, :, j], in_=planes[j - 2][:].indirect(offsets[:, j0 // 16 : j1 // 16]))
+            nc.vector.tensor_copy(out=picked[:, :, j], in_=planes[j][:].indirect(offsets[:, j0 // 16 : j1 // 16]))
 
         def quantize(h):
             nc.vector.quantize_mx(out=x_codes[h][:].bitcast(FP8X4), scales=x_scales[h][:], in_=picks[h])
@@ -159,23 +135,21 @@ def tile_picked_pool_lin_relu_sub_e_kernel(tc, xT, w, b, offs, out):
                 op1=MAX,
             )
 
-        cast_pairs(0)
-        cast_pairs(1)
-        gather_pairs(0, HALF, picks[0])
-        gather_pairs(HALF, S, picks[1])
-        gather_plane(2, 0, HALF, picks[0])
-        gather_plane(2, HALF, S, picks[1])
+        for j in range(3):
+            gather_plane(j, 0, HALF, picks[0])
+            gather_plane(j, HALF, S, picks[1])
         gather_plane(3, 0, HALF, picks[0])
-        w_groups = [cast_w(0, shared[:, 0:W_WIDE]), cast_w(1, w_last[:])]
+        w_groups = [cast_w(0, shared[:, 0:W_WIDE]), cast_w(1, w_rest[0][:]), cast_w(2, w_rest[1][:])]
         quantize(0)
         quantize_w(0, w_groups[0])
         multiply(0, 0)
-        multiply(0, 1)
         for t in range(2):
             sums[1, 2 + t] = psum.tile([P, VH, D], F32, name=f"acc1{2 + t}")
-            multiply(0, t, sums[1, 2 + t])
+            multiply(0, 0, sums[1, 2 + t])
         gather_plane(3, HALF - 32, S, shared[:, W_WIDE - 32 * 4 :])
         quantize_w(1, w_groups[1])
+        multiply(0, 1)
+        quantize_w(2, w_groups[2])
         multiply(0, 2)
         multiply(0, 3)
         quantize(1)
@@ -193,5 +167,7 @@ def tile_picked_pool_lin_relu_sub_e_kernel(tc, xT, w, b, offs, out):
         finish(1, 0, 2)
         store(1, 0, 2)
         pool_pairs(1, 3)
-        finish(1, 2, 4)
-        store(1, 2, 4)
+        finish(1, 2, 3)
+        store(1, 2, 3)
+        finish(1, 3, 4)
+        store(1, 3, 4)

from contextlib import ExitStack

import concourse.mybir as mybir

K, T, D, S, N = 512, 4096, 4, 1024, 512
V = S // D
FLOPS = 2 * K * N * S

F32 = mybir.dt.float32
BF16 = mybir.dt.bfloat16
U32 = mybir.dt.uint32
U16 = mybir.dt.uint16
U8 = mybir.dt.uint8
FP8X4 = mybir.dt.float8_e4m3fn_x4
COPY = mybir.ActivationFunctionType.Copy
IDENTITY = mybir.ActivationFunctionType.Identity
ADD = mybir.AluOpType.add
MAX = mybir.AluOpType.max

P = 128
HALF = S // 2
VH = V // 2
MT = N // P


def tile_picked_pool_lin_relu_sub_e_kernel(tc, xT, w, b, offs, out):
    nc = tc.nc
    with ExitStack() as ctx:
        keep = ctx.enter_context(tc.tile_pool(name="keep", bufs=1))
        psum = ctx.enter_context(tc.psum_pool(name="psum", bufs=1))

        offsets = keep.tile([P, S // 16], U16, name="offsets")
        nc.sync.dma_start(offsets[:], offs)
        bias = keep.tile([P, MT], F32, name="bias")

        x_rows = xT.rearrange("(p j) n -> p j n", j=4)
        w_rows = w.rearrange("(p j) m -> p j m", j=4)
        pieces = ((0, 128), (128, 256), (256, 512))
        w_codes, w_scales = [], []

        def load_w(c0, c1, name):
            r = keep.tile([P, 4, c1 - c0], F32, name=name)
            nc.sync.dma_start(out=r[:], in_=w_rows[:, :, c0:c1])
            return r

        def cast_w(i, g):
            view = g.rearrange("p (m j) -> p m j", j=4)
            nc.scalar.activation(out=view, in_=w_raws[i].rearrange("p j m -> p m j"), func=COPY)
            return g

        def quantize_w(i, g):
            c0, c1 = pieces[i]
            codes = keep.tile([P, c1 - c0], U32, name=f"w_codes{i}", align_bytes=64)
            scales = keep.tile([P, c1 - c0], U8, name=f"w_scales{i}", align_bytes=64)
            nc.vector.quantize_mx(
                out=codes[:].bitcast(FP8X4), scales=scales[:], in_=g
            )
            w_codes.append(codes)
            w_scales.append(scales)

        planes = []
        for j in range(4):
            r = keep.tile([P, T], F32, name=f"plane{j}")
            nc.sync.dma_start(out=r[:], in_=x_rows[:, j, :])
            planes.append(r)
        w_front = load_w(0, 256, "w_front")
        w_back = load_w(256, 512, "w_back")
        w_raws = [w_front[:, :, 0:128], w_front[:, :, 128:256], w_back[:]]
        nc.sync.dma_start(out=bias[:], in_=b.rearrange("(t p) o -> p (t o)", p=P))

        W_WIDE = 128 * 4
        X_WIDE = HALF * 4
        picks0 = keep.tile([P, X_WIDE], BF16, name="picks0", align_bytes=64)
        shared = keep.tile([P, W_WIDE + X_WIDE], BF16, name="shared", align_bytes=64)
        w_rest = [keep.tile([P, n * 4], BF16, name=f"w_rest{n}", align_bytes=64) for n in (128, 256)]
        picks = [picks0[:], shared[:, W_WIDE:]]
        x_codes = [keep.tile([P, HALF], U32, name=f"x_codes{h}", align_bytes=64) for h in range(2)]
        x_scales = [keep.tile([P, HALF], U8, name=f"x_scales{h}", align_bytes=64) for h in range(2)]

        def gather_plane(j, j0, j1, where):
            picked = where.rearrange("p (n t) -> p n t", t=4)
            nc.vector.tensor_copy(out=picked[:, :, j], in_=planes[j][:].indirect(offsets[:, j0 // 16 : j1 // 16]))

        def quantize(h):
            nc.vector.quantize_mx(out=x_codes[h][:].bitcast(FP8X4), scales=x_scales[h][:], in_=picks[h])

        sums = {}

        def multiply(h, t, into=None):
            acc = into or psum.tile([P, VH, D], F32, name=f"acc{h}{t}")
            i = [k for k, (c0, c1) in enumerate(pieces) if c0 <= t * P < c1][0]
            cols = slice(t * P - pieces[i][0], t * P - pieces[i][0] + P)
            nc.tensor.matmul_mx(
                out=acc[:].rearrange("p v d -> p (v d)"),
                lhsT=w_codes[i][:, cols].bitcast(FP8X4),
                lhsT_scale=w_scales[i][:, cols],
                rhs=x_codes[h][:].bitcast(FP8X4),
                rhs_scale=x_scales[h][:],
                start=True,
                stop=True,
            )
            if not into:
                sums[h, t] = acc

        out_view = out.rearrange("(t p) v -> p t v", p=P)
        halves = [keep.tile([P, MT, VH, 2], F32, name=f"halves{h}") for h in range(2)]
        best = [keep.tile([P, MT, VH], F32, name=f"best{h}") for h in range(2)]
        first = [keep.tile([P, MT, VH, 2], F32, name=f"first{h}") for h in range(2)]

        def pool_pairs(h, t):
            acc = sums[h, t]
            nc.scalar.activation(
                out=first[h][:, t, :, :], in_=acc[:, :, 0:2], func=IDENTITY, bias=bias[:, t : t + 1], scale=1.0
            )
            nc.vector.scalar_tensor_tensor(
                out=halves[h][:, t, :, :],
                in0=acc[:, :, 2:4],
                scalar=bias[:, t : t + 1],
                in1=first[h][:, t, :, :],
                op0=ADD,
                op1=MAX,
            )

        def store(h, t0, t1):
            nc.sync.dma_start(out=out_view[:, t0:t1, h * VH : (h + 1) * VH], in_=best[h][:, t0:t1, :])

        def finish(h, t0, t1):
            some = slice(t0, t1)
            nc.vector.scalar_tensor_tensor(
                out=best[h][:, some, :],
                in0=halves[h][:, some, :, 0],
                scalar=0.0,
                in1=halves[h][:, some, :, 1],
                op0=MAX,
                op1=MAX,
            )

        for j in range(3):
            gather_plane(j, 0, HALF, picks[0])
            gather_plane(j, HALF, S, picks[1])
        gather_plane(3, 0, HALF, picks[0])
        w_groups = [cast_w(0, shared[:, 0:W_WIDE]), cast_w(1, w_rest[0][:]), cast_w(2, w_rest[1][:])]
        quantize(0)
        quantize_w(0, w_groups[0])
        multiply(0, 0)
        for t in range(2):
            sums[1, 2 + t] = psum.tile([P, VH, D], F32, name=f"acc1{2 + t}")
            multiply(0, 0, sums[1, 2 + t])
        gather_plane(3, HALF - 32, S, shared[:, W_WIDE - 32 * 4 :])
        quantize_w(1, w_groups[1])
        multiply(0, 1)
        quantize_w(2, w_groups[2])
        multiply(0, 2)
        multiply(0, 3)
        quantize(1)
        multiply(1, 0)
        multiply(1, 1)
        multiply(1, 2, sums[1, 2])
        multiply(1, 3, sums[1, 3])
        for t in range(MT):
            pool_pairs(0, t)
        pool_pairs(1, 0)
        finish(0, 0, 4)
        store(0, 0, 4)
        pool_pairs(1, 1)
        pool_pairs(1, 2)
        finish(1, 0, 2)
        store(1, 0, 2)
        pool_pairs(1, 3)
        finish(1, 2, 3)
        store(1, 2, 3)
        finish(1, 3, 4)
        store(1, 3, 4)
